import numpy as np
import ml_dtypes

BF16 = ml_dtypes.bfloat16


def bf(x):
    return np.asarray(x, np.float32).astype(BF16)


def f32(x):
    return np.asarray(x, np.float32)


def f64(x):
    return np.asarray(x).astype(np.float64)


def striped(idx):
    return np.tile(idx.reshape(-1, 16).T, (8, 1))


S, K, M, N = 2048, 128, 128, 2048


def setup_inputs():
    return {"table": bf(np.random.standard_normal((K, S))), "w": bf(np.random.standard_normal((K, M)) / np.sqrt(K)), "b": f32(0.5 * np.random.standard_normal((M, 1))), "offs": striped(np.random.permutation(S))}


def reference(table, w, b, offs):
    idx = offs[:16].T.reshape(-1)
    x = f64(table)[:, idx]
    y = f64(w).T @ x
    return np.maximum(y + f64(b), 0.0)

@@ -1,0 +1,62 @@
+import concourse.mybir as mybir
+
+BF16, F32, U16 = mybir.dt.bfloat16, mybir.dt.float32, mybir.dt.uint16
+RELU = mybir.ActivationFunctionType.Relu
+ADD, MAX = mybir.AluOpType.add, mybir.AluOpType.max
+
+P = 128
+TOKENS = 2048
+STORE = 256
+PER_COLUMN = 16
+BANKS = 8
+
+FLOPS = 2 * P * P * TOKENS
+
+
+def tile_gather_matmul_kernel(tc, table, w, b, offs, out):
+    nc = tc.nc
+    half = TOKENS // 2
+    with (
+        tc.tile_pool(name="held", bufs=1) as held,
+        tc.tile_pool(name="results", bufs=TOKENS // STORE) as results,
+        tc.psum_pool(name="banks", bufs=BANKS) as banks,
+    ):
+        offsets = held.tile([P, TOKENS // PER_COLUMN], U16, name="offsets")
+        tokens = held.tile([P, TOKENS], BF16, name="tokens")
+        weights = held.tile([P, P], BF16, name="weights")
+        bias = held.tile([P, 1], F32, name="bias")
+        nc.sync.dma_start(offsets[:], offs)
+        nc.scalar.dma_start(tokens[:, 0:half], table[:, 0:half])
+        nc.sync.dma_start(weights[:], w)
+        nc.sync.dma_start(tokens[:, half:TOKENS], table[:, half:TOKENS])
+        nc.scalar.dma_start(bias[:], b)
+
+        zeros = held.tile([P, 1], BF16, name="zeros")
+        nc.vector.memset(zeros[:], 0.0)
+        early = held.tile([P, 1], BF16, name="early")
+        nc.scalar.activation(early[:], zeros[:], RELU)
+
+        stores = TOKENS // STORE
+        piece = 0
+        for store in range(stores):
+            at_an_end = store == 0 or store == stores - 1
+            width = STORE // 2 if at_an_end else STORE
+            result = results.tile([P, STORE], F32, name="result")
+            for left in range(0, STORE, width):
+                first = store * STORE + left
+                bank = banks.tile([P, width], F32, name="bank")
+                picked = tokens[:].indirect(
+                    offsets[:, first // PER_COLUMN : (first + width) // PER_COLUMN]
+                )
+                nc.tensor.matmul(bank[:], weights[:], picked, start=True, stop=True)
+
+                if piece % 2 == 0:
+                    nc.scalar.activation(
+                        result[:, left : left + width], bank[:], RELU, bias=bias[:, 0:1]
+                    )
+                else:
+                    nc.vector.tensor_scalar(
+                        result[:, left : left + width], bank[:], bias[:, 0:1], 0.0, ADD, MAX
+                    )
+                piece += 1
+            nc.sync.dma_start(out[:, store * STORE : (store + 1) * STORE], result[:])

@@ -15,7 +15,6 @@ FLOPS = 2 * P * P * TOKENS
 
 def tile_gather_matmul_kernel(tc, table, w, b, offs, out):
     nc = tc.nc
-    half = TOKENS // 2
     with (
         tc.tile_pool(name="held", bufs=1) as held,
         tc.tile_pool(name="results", bufs=TOKENS // STORE) as results,
@@ -25,11 +24,10 @@ def tile_gather_matmul_kernel(tc, table, w, b, offs, out):
         tokens = held.tile([P, TOKENS], BF16, name="tokens")
         weights = held.tile([P, P], BF16, name="weights")
         bias = held.tile([P, 1], F32, name="bias")
+        nc.sync.dma_start(tokens[:], table)
         nc.sync.dma_start(offsets[:], offs)
-        nc.scalar.dma_start(tokens[:, 0:half], table[:, 0:half])
         nc.sync.dma_start(weights[:], w)
-        nc.sync.dma_start(tokens[:, half:TOKENS], table[:, half:TOKENS])
-        nc.scalar.dma_start(bias[:], b)
+        nc.sync.dma_start(bias[:], b)
 
         zeros = held.tile([P, 1], BF16, name="zeros")
         nc.vector.memset(zeros[:], 0.0)

@@ -6,7 +6,8 @@ ADD, MAX = mybir.AluOpType.add, mybir.AluOpType.max
 
 P = 128
 TOKENS = 2048
-STORE = 256
+PIECE = 256
+STORE = 2 * PIECE
 PER_COLUMN = 16
 BANKS = 8
 
@@ -34,27 +35,23 @@ def tile_gather_matmul_kernel(tc, table, w, b, offs, out):
         early = held.tile([P, 1], BF16, name="early")
         nc.scalar.activation(early[:], zeros[:], RELU)
 
-        stores = TOKENS // STORE
-        piece = 0
-        for store in range(stores):
-            at_an_end = store == 0 or store == stores - 1
-            width = STORE // 2 if at_an_end else STORE
+        for store in range(TOKENS // STORE):
             result = results.tile([P, STORE], F32, name="result")
-            for left in range(0, STORE, width):
+            for piece in range(STORE // PIECE):
+                left = piece * PIECE
                 first = store * STORE + left
-                bank = banks.tile([P, width], F32, name="bank")
+                bank = banks.tile([P, PIECE], F32, name="bank")
                 picked = tokens[:].indirect(
-                    offsets[:, first // PER_COLUMN : (first + width) // PER_COLUMN]
+                    offsets[:, first // PER_COLUMN : (first + PIECE) // PER_COLUMN]
                 )
                 nc.tensor.matmul(bank[:], weights[:], picked, start=True, stop=True)
 
                 if piece % 2 == 0:
                     nc.scalar.activation(
-                        result[:, left : left + width], bank[:], RELU, bias=bias[:, 0:1]
+                        result[:, left : left + PIECE], bank[:], RELU, bias=bias[:, 0:1]
                     )
                 else:
                     nc.vector.tensor_scalar(
-                        result[:, left : left + width], bank[:], bias[:, 0:1], 0.0, ADD, MAX
+                        result[:, left : left + PIECE], bank[:], bias[:, 0:1], 0.0, ADD, MAX
                     )
-                piece += 1
             nc.sync.dma_start(out[:, store * STORE : (store + 1) * STORE], result[:])

@@ -35,23 +35,26 @@ def tile_gather_matmul_kernel(tc, table, w, b, offs, out):
         early = held.tile([P, 1], BF16, name="early")
         nc.scalar.activation(early[:], zeros[:], RELU)
 
-        for store in range(TOKENS // STORE):
-            result = results.tile([P, STORE], F32, name="result")
-            for piece in range(STORE // PIECE):
-                left = piece * PIECE
-                first = store * STORE + left
-                bank = banks.tile([P, PIECE], F32, name="bank")
-                picked = tokens[:].indirect(
-                    offsets[:, first // PER_COLUMN : (first + PIECE) // PER_COLUMN]
-                )
-                nc.tensor.matmul(bank[:], weights[:], picked, start=True, stop=True)
+        widths = [PIECE] * (TOKENS // PIECE - 1) + [PIECE // 2] * 2
+        first = 0
+        for piece, width in enumerate(widths):
+            left = first % STORE
+            if left == 0:
+                result = results.tile([P, STORE], F32, name="result")
+            bank = banks.tile([P, width], F32, name="bank")
+            picked = tokens[:].indirect(
+                offsets[:, first // PER_COLUMN : (first + width) // PER_COLUMN]
+            )
+            nc.tensor.matmul(bank[:], weights[:], picked, start=True, stop=True)
 
-                if piece % 2 == 0:
-                    nc.scalar.activation(
-                        result[:, left : left + PIECE], bank[:], RELU, bias=bias[:, 0:1]
-                    )
-                else:
-                    nc.vector.tensor_scalar(
-                        result[:, left : left + PIECE], bank[:], bias[:, 0:1], 0.0, ADD, MAX
-                    )
-            nc.sync.dma_start(out[:, store * STORE : (store + 1) * STORE], result[:])
+            if piece % 2 == 1:
+                nc.scalar.activation(
+                    result[:, left : left + width], bank[:], RELU, bias=bias[:, 0:1]
+                )
+            else:
+                nc.vector.tensor_scalar(
+                    result[:, left : left + width], bank[:], bias[:, 0:1], 0.0, ADD, MAX
+                )
+            first += width
+            if first % STORE == 0:
+                nc.sync.dma_start(out[:, first - STORE : first], result[:])

@@ -25,10 +25,10 @@ def tile_gather_matmul_kernel(tc, table, w, b, offs, out):
         tokens = held.tile([P, TOKENS], BF16, name="tokens")
         weights = held.tile([P, P], BF16, name="weights")
         bias = held.tile([P, 1], F32, name="bias")
-        nc.sync.dma_start(tokens[:], table)
         nc.sync.dma_start(offsets[:], offs)
         nc.sync.dma_start(weights[:], w)
-        nc.sync.dma_start(bias[:], b)
+        nc.scalar.dma_start(tokens[:], table)
+        nc.scalar.dma_start(bias[:], b)
 
         zeros = held.tile([P, 1], BF16, name="zeros")
         nc.vector.memset(zeros[:], 0.0)

@@ -35,7 +35,7 @@ def tile_gather_matmul_kernel(tc, table, w, b, offs, out):
         early = held.tile([P, 1], BF16, name="early")
         nc.scalar.activation(early[:], zeros[:], RELU)
 
-        widths = [PIECE] * (TOKENS // PIECE - 1) + [PIECE // 2] * 2
+        widths = [PIECE, PIECE // 2, PIECE // 2] * (TOKENS // STORE)
         first = 0
         for piece, width in enumerate(widths):
             left = first % STORE

import concourse.mybir as mybir

BF16, F32, U16 = mybir.dt.bfloat16, mybir.dt.float32, mybir.dt.uint16
RELU = mybir.ActivationFunctionType.Relu
ADD, MAX = mybir.AluOpType.add, mybir.AluOpType.max

P = 128
TOKENS = 2048
PIECE = 256
STORE = 2 * PIECE
PER_COLUMN = 16
BANKS = 8

FLOPS = 2 * P * P * TOKENS


def tile_gather_matmul_kernel(tc, table, w, b, offs, out):
    nc = tc.nc
    with (
        tc.tile_pool(name="held", bufs=1) as held,
        tc.tile_pool(name="results", bufs=TOKENS // STORE) as results,
        tc.psum_pool(name="banks", bufs=BANKS) as banks,
    ):
        offsets = held.tile([P, TOKENS // PER_COLUMN], U16, name="offsets")
        tokens = held.tile([P, TOKENS], BF16, name="tokens")
        weights = held.tile([P, P], BF16, name="weights")
        bias = held.tile([P, 1], F32, name="bias")
        nc.sync.dma_start(offsets[:], offs)
        nc.sync.dma_start(weights[:], w)
        nc.scalar.dma_start(tokens[:], table)
        nc.scalar.dma_start(bias[:], b)

        zeros = held.tile([P, 1], BF16, name="zeros")
        nc.vector.memset(zeros[:], 0.0)
        early = held.tile([P, 1], BF16, name="early")
        nc.scalar.activation(early[:], zeros[:], RELU)

        widths = [PIECE, PIECE // 2, PIECE // 2] * (TOKENS // STORE)
        first = 0
        for piece, width in enumerate(widths):
            left = first % STORE
            if left == 0:
                result = results.tile([P, STORE], F32, name="result")
            bank = banks.tile([P, width], F32, name="bank")
            picked = tokens[:].indirect(
                offsets[:, first // PER_COLUMN : (first + width) // PER_COLUMN]
            )
            nc.tensor.matmul(bank[:], weights[:], picked, start=True, stop=True)

            if piece % 2 == 1:
                nc.scalar.activation(
                    result[:, left : left + width], bank[:], RELU, bias=bias[:, 0:1]
                )
            else:
                nc.vector.tensor_scalar(
                    result[:, left : left + width], bank[:], bias[:, 0:1], 0.0, ADD, MAX
                )
            first += width
            if first % STORE == 0:
                nc.sync.dma_start(out[:, first - STORE : first], result[:])
